import numpy as np, ml_dtypes
CORES = [40,41,42,43,44,45,46,47]
N = 8
import mx_ref
BF = ml_dtypes.bfloat16
def gentries(a):
    return np.ascontiguousarray(a.reshape(8, 16, -1).transpose(0, 2, 1)).reshape(8, -1)
def gtable(e):
    e = np.asarray(e); return np.ascontiguousarray(e.reshape(8, -1, 16).transpose(0, 2, 1)).reshape(128, -1).astype(np.int32)
def gcols(t, e):
    v = np.concatenate([t.reshape(8, 16, -1, 4), np.zeros((8, 16, 1, 4), BF)], axis=2)
    return np.ascontiguousarray(np.stack([v[g][:, e[g]] for g in range(8)])).reshape(128, -1)
def tile(rs):
    return np.stack(rs, axis=2).reshape(128, -1).astype(BF)
def cut(t, i, w=512):
    return t[:, w * i:w * i + w]
def pick(q, e):
    c = np.concatenate([q[0].reshape(128, -1, 4), np.zeros((128, 1, 4), np.uint8)], axis=1); s = np.concatenate([q[1], np.ones((16, 1), np.uint8)], axis=1)
    return (np.ascontiguousarray(c[:, e].reshape(128, -1)), np.ascontiguousarray(s[:, e]))
def join(*qs):
    return (np.concatenate([q[0] for q in qs], axis=1), np.concatenate([q[1] for q in qs], axis=1))
def put(q, e, v):
    c, s = q[0].reshape(128, -1, 4).copy(), q[1].copy(); c[:, e] = v[0].reshape(128, -1, 4); s[:, e] = v[1]
    return (c.reshape(128, -1), s)
def pk(c, s):
    return (np.ascontiguousarray(c), mx_ref.live(s))
def emit(q):
    return q[0], q[1]
def packed(v, rng):
    q = [mx_ref.quantize(np.ascontiguousarray(v[r])) for r in range(N)]
    return np.stack([a for a, b in q]), np.stack([mx_ref.plane(b, rng) for a, b in q])
def values_of_codes():
    e, c = np.zeros((128, 128, 4), np.float32), np.zeros((128, 2, 4), np.uint8)
    e[np.arange(128), np.arange(128), 0] = 1
    c[:127, :, 0] = np.arange(256).reshape(2, 128).T[:127]
    return mx_ref.matmul(mx_ref.quantize(e.reshape(128, 512).astype(BF)), (c.reshape(128, 8), np.full((16, 2), 127, np.uint8))).T.reshape(-1).astype(np.float64)
CODE_VALUE, SCALE_VALUE = values_of_codes(), 2.0 ** (np.arange(256) - 127.0)
def decode(q):
    return (CODE_VALUE[q[0]].reshape(16, 8, -1, 4) * SCALE_VALUE[q[1]][:, None, :, None] + 0.0).reshape(128, -1).astype(np.float32)
def f(rng, *shape):
    return mx_ref.flush((rng.standard_normal(shape, dtype=np.float32) * np.exp2(rng.integers(-2, 3, shape[:-1] + (1,)))).astype(BF))
def wide(rng, *shape, cols=0):
    v = rng.standard_normal(shape, dtype=np.float32) * np.exp2(rng.integers(-12, 13, shape)).astype(np.float32)
    if cols: v *= np.repeat(np.exp2(rng.integers(-cols, cols + 1, shape[:-2] + (1, shape[-1] // 4))) * (rng.random(shape[:-2] + (1, shape[-1] // 4)) > 0.0625), 4, axis=-1).astype(np.float32)
    return mx_ref.flush(v.astype(BF))
C, S = 256, 48
def stored(j):
    e = j.reshape(2, 8, N, C).transpose(2, 1, 0, 3).reshape(N, 8, 2 * C)
    return np.stack([gtable(e[r]) for r in range(N)])
def both(a):
    return np.stack([gentries(a[r]) for r in range(N)]).reshape(N, 8, 2, C).transpose(2, 1, 0, 3).reshape(2, 8, N * C)
def seats(rng):
    p = rng.permutation(N)
    return p, [np.stack([rng.permutation(C) for r in range(N)]) for h in range(3)]
def place(rng, s, u, seat=None, bits=False):
    p, w = seat or seats(rng)
    n = []
    for h, o in zip((np.zeros(C, int), np.array(s), np.array(u)), w):
        b = p[np.arange(N)[:, None] ^ h if bits else (np.arange(N)[:, None] + h) % N]
        n.append(C * b + o[b, np.arange(C)])
    j, k = np.zeros(N * C, int), np.zeros(N * C, int)
    j[n[0]], k[n[0]] = n[1], n[2]
    return j, k
def roam(rng):
    s, u = [0] * C, [0] * C
    n = [[0] * N for k in range(3)]
    n[0][0] = n[1][0] = n[2][0] = C
    def add(a, b, w):
        n[0][a] += w
        n[1][b] += w
        n[2][(b - a) % N] += w
    for t, a, b in zip(rng.integers(0, C, 6 * C).tolist(), rng.integers(0, N, 6 * C).tolist(), rng.integers(0, N, 6 * C).tolist()):
        add(s[t], u[t], -1)
        add(a, b, 1)
        if max(max(m[1:]) for m in n) <= S:
            s[t], u[t] = a, b
        else:
            add(a, b, -1)
            add(s[t], u[t], 1)
    return s, u
def brim(rng, kind):
    s = np.zeros(C, int)
    m = np.repeat(1 + rng.permutation(N - 1), S)[:C]
    s[:len(m)] = m
    z = np.zeros(C, int)
    return ((s, s), (s, z), (z, s), (z, z))[kind]
def apart(n):
    x = np.array({4: [1, 2, 3], 8: [1, 2, 4, 3, 6, 7, 5]}[N])
    t = np.arange(C)
    return [np.where(t < 256, x[(t + h) % (N - 1)], 0) for h in ((0, 1), (3, 2))[n]]
def lists_of(rng, steps):
    e = [[place(rng, *steps[n][g]) for g in range(8)] for n in range(2)]
    return np.array([[p[0] for p in h] for h in e]), np.array([[p[1] for p in h] for h in e])
def big(v, k, low=-12):
    v = v.astype(np.float32) * np.float32(k)
    v[np.abs(v) < np.float32(2.0 ** low)] = 0
    return v.astype(BF)
def weights(rng, k, low=-20):
    c, p = packed(big(f(rng, N, 128, 2048), k, low), rng)
    return {"wc": c, "ws": p}
def numbers_of(rng):
    return {"xb": big(f(rng, N, 128, 4 * C), 1), "xc": big(f(rng, N, 128, 4 * C), 1), "v": np.array(f(rng, N, 128, 512))}
def with_lists(d, jk):
    return {**d, "jb": stored(jk[0]), "kc": stored(jk[1])}
def setup_inputs(rng):
    d = {**numbers_of(rng), **weights(rng, 0.25)}
    return with_lists(d, lists_of(rng, [[roam(rng) for g in range(8)] for n in range(2)]))
def setup_inputs_full(rng):
    d = {**numbers_of(rng), **weights(rng, 0.25)}
    return with_lists(d, lists_of(rng, [[brim(rng, k % 4) for k in rng.permutation(8)] for n in range(2)]))
def setup_inputs_shared(rng):
    d = {**numbers_of(rng), **weights(rng, 0.25)}
    s, u = np.zeros(C, int), np.zeros(C, int)
    s[:3 * S] = np.repeat([1, 2, N - 1], S)
    u[:2 * S] = np.repeat([3, 1], S)
    e = []
    for far in rng.permutation(8) % 2:
        p, w = seats(rng)
        if far:
            e.append([place(rng, *apart(n), (p, [np.roll(o, n * 256, axis=1) for o in w]), True) for n in range(2)])
        else:
            e.append([place(rng, s, u, (p, w)), place(rng, s, u, (p, [np.roll(o, 2 * S, axis=1) for o in w]))])
    return with_lists(d, np.array(e).transpose(2, 1, 0, 3))
def setup_inputs_twins(rng):
    d = {**numbers_of(rng), **weights(rng, 0.25)}
    e = [roam(rng) for g in range(8)]
    j, k = lists_of(rng, [e, e])
    g = (rng.permutation(8) % 2 == 0)[:, None]
    j[1], k[1] = np.where(g, j[0], k[0]), np.where(g, k[0], j[0])
    return with_lists(d, (j, k))
def setup_inputs_gaps(rng):
    d = setup_inputs(rng)
    e = rng.permutation(N)
    d["xb"][e[0]] = 0
    d["xc"][e[1]] = np.tile(d["xc"][e[1]][:, :4], (1, C))
    g = int(rng.integers(8))
    d["xc"][e[2], 16 * g:16 * g + 16] = 0
    return d
def setup_inputs_spread(rng):
    d = {**setup_inputs(rng), **weights(rng, 2.0 ** -8, -24)}
    for n in ("xb", "xc"): d[n] = big(wide(rng, N, 128, 4 * C, cols=3), 2.0 ** -6)
    return d
def check_inputs(d):
    b = []
    for k in ("xb", "xc", "v"):
        a = np.abs(d[k].astype(np.float32))
        if not (np.isfinite(a).all() and ((a == 0) | (a >= 2.0 ** -30) & (a <= 2.0 ** 30)).all()): b.append("a value of " + k)
    e = {k: both(d[k]) for k in ("jb", "kc")}
    for k in ("jb", "kc"):
        if (np.sort(e[k], axis=2) != np.arange(N * C)).any(): b.append("a number that isn't there exactly once in a half and group of " + k)
    if any(((e[k] < 0) | (e[k] >= N * C)).any() for k in e): return b
    own = np.arange(N * C) // C
    over = set()
    for n in range(2):
        for g in range(8):
            j, k = e["jb"][n, g] // C, e["kc"][n, g] // C
            for name, p, q in (("A and B", own, j), ("A and C", own, k), ("B and C", j, k)):
                c = np.bincount(N * p + q, minlength=N * N).reshape(N, N)
                np.fill_diagonal(c, 0)
                if c.max() > S: over.add("too many nonzeros between two ranks: " + name)
    return b + sorted(over)
def held(q):
    return decode(join(*q)).astype(BF)
def pairs(p, q, e, h):
    a, b = [gcols(p, e[n]).astype(np.float32) * gcols(q, h[n]).astype(np.float32) for n in range(2)]
    return (a + b).astype(BF)
def layer(lay, m):
    o = []
    for r in range(N):
        q = mx_ref.quantize(np.ascontiguousarray(cut(m, r, 4 * C)))
        o.append(mx_ref.quantize(tile([mx_ref.matmul(pick(lay[r], np.arange(128 * b, 128 * b + 128)), q) * np.float32(0.03125) for b in range(4)])))
    return o
def reference(xb, xc, v, wc, ws, jb, kc):
    lay = [pk(wc[r], ws[r]) for r in range(N)]
    j, k = both(jb), both(kc)
    oldb = held([mx_ref.quantize(xb[r]) for r in range(N)])
    oldc = held([mx_ref.quantize(xc[r]) for r in range(N)])
    qa = layer(lay, pairs(oldb, oldc, j, k))
    newa = held(qa)
    i = np.argsort(j, axis=2)
    qb = layer(lay, pairs(newa, oldc, i, np.take_along_axis(k, i, axis=2)))
    newb = held(qb)
    i = np.argsort(k, axis=2)
    qc = layer(lay, pairs(newa, newb, i, np.take_along_axis(j, i, axis=2)))
    y = np.zeros((N, 128, 3 * C), np.float32)
    oc, osc = np.zeros((N, 128, 12 * C), np.uint8), np.zeros((N, 16, 3 * C), np.uint8)
    for r in range(N):
        q = join(qa[r], qb[r], qc[r])
        y[r] = mx_ref.matmul(mx_ref.quantize(v[r]), q)
        oc[r], osc[r] = emit(q)
    return {"y": y, "oc": oc, "osc": osc}

@@ -1,0 +1,663 @@
+from concourse.bass import DstId, RemoteDMATransfer
+from concourse.mybir import dt, AluOpType, ActivationFunctionType
+
+N, C, S = 8, 256, 48
+B = 2 * S
+L = (N - 1) * B
+K = L // 16
+WQ = 2 * L
+WIN = WQ + 512 + 32 + WQ + 32
+PAD = 4096.0
+F32, BF, I32, U16, X4, U8 = "float32", "bfloat16", "int32", "uint16", "float8_e4m3fn_x4", "uint8"
+BYTES = {F32: 4, I32: 4, X4: 4, BF: 2, U16: 2, U8: 1}
+
+SCRATCH = {}
+
+
+def _sb(names, n, t):
+    for x in names.split():
+        SCRATCH[x] = ("sbuf", [128, n], t)
+
+
+_sb("jn kn", 32, I32)
+_sb("flat", 512, I32)
+_sb("xbt xct xbp nt0 nt1 nt2 mt", 1024, BF)
+_sb("vt zb", 512, BF)
+_sb("gs0 gs1 gs2 pr", 2048, BF)
+_sb("eb", 4 * 516, BF)
+_sb("ct0 ct1", 4 * L, BF)
+for _n, _w in (("w", 512), ("v", 128), ("e", 1024), ("c0", N * C), ("a", N * C), ("b0", L + C), ("b1", L + C), ("c1", C),
+               ("m0", C), ("m1", C), ("m2", C), ("t0", L), ("t1", L),
+               ("p0", 1024), ("p1", 1024), ("p2", 1024), ("p3", 1024), ("p4", 1024), ("p5", 1024)):
+    _sb(_n + "q", _w, X4)
+    _sb(_n + "z", _w, U8)
+_sb("idt", 128, F32)
+_sb("cf", 768, F32)
+_sb("ci", 192, I32)
+_sb("cu", 64, U16)
+_sb("rf", 7168, F32)
+_sb("ri", 1024, I32)
+_sb("ru", 1024, U16)
+_sb("win0 win1", WIN, F32)
+_sb("wt0", WQ, F32)
+_sb("fr0 fr1 fl0 fl1", L, F32)
+_sb("rq0 rl0", 3 * K, F32)
+_sb("rq1 rl1", 2 * K, U16)
+_sb("ysb", 3 * C, F32)
+for _k in range(8):
+    SCRATCH["ps%d" % _k] = ("psum", [128, 512], F32)
+
+ARR = ["c0q", "c0z", "aq", "az", "b0q", "b0z", "b1q", "b1z", "far0", "near0", "all1"]
+SEMAPHORES = ["qv", "qs", "qt", "qg", "sent"] + ["in_" + x for x in ARR] + ["d%d" % k for k in range(40)]
+
+A = AluOpType
+COPY = ActivationFunctionType.Copy
+IDENT = ActivationFunctionType.Identity
+WAKE, LOCAL, REMOTE, FIRST, ROW, RATE, GATHER, SCATTER = 70.0, 2000.0, 2000.0, 3200.0, 25.0, 20.0, 1.62, 3.9
+
+
+def rank_program(g, core, T, topo):
+    r = T.rank_of(core)
+    if r is None:
+        return
+    cores = T.cores
+
+    def order(a):
+        o = [x for x in range(N) if x != a]
+        return [x for x in o if topo.die(cores[x]) != topo.die(cores[a])] + [x for x in o if topo.die(cores[x]) == topo.die(cores[a])]
+
+    others = order(r)
+    nx = len([x for x in others if topo.die(cores[x]) != topo.die(core)])
+    eng = topo.engines(core, cores[others[0]])
+    even, odd = eng[0::2], eng[1::2]
+
+    Q = {"v": g.vector, "s": g.scalar, "t": g.tensor, "g": g, "y": g.sync}
+    count, seen, log, ndma, nodes, tail, sent = {}, {}, {}, [0], [], {}, {}
+
+    def R(name, a=None, b=None, s=1, p=None):
+        if a is None:
+            a, b = 0, T[name].shape[1]
+        cs = slice(a, b, s) if s > 1 else slice(a, b)
+        ap = T[name][:, cs] if p is None else T[name][slice(p[0], p[1], p[2]), cs]
+        if name[:2] == "ps":
+            return ap, [(name, 0, 512, 1, None, b - a)]
+        return ap, [(name, a, b, s, p, (b - a + s - 1) // s)]
+
+    def ext(ap):
+        return ap, []
+
+    def u8(x):
+        return x[0].bitcast(dt.uint8), x[1]
+
+    def u32(x):
+        return x[0].bitcast(dt.uint32), x[1]
+
+    def ind(w, o):
+        return w[0].indirect(o[0]), w[1], o[1]
+
+    def meet(x, y):
+        if x[2] <= y[1] or y[2] <= x[1]:
+            return False
+        if x[3] > 1 and x[3] == y[3] and x[1] % x[3] != y[1] % y[3]:
+            return False
+        if x[4] and y[4] and not set(range(*x[4])) & set(range(*y[4])):
+            return False
+        return True
+
+    def wait(q, tok):
+        if seen.get((q, tok[0]), 0) < tok[1]:
+            seen[(q, tok[0])] = tok[1]
+            Q[q].wait_ge(T.sem[tok[0]], tok[1])
+
+    def node(q, reads, writes, cost, lag, call, more=(), move=None):
+        need, follow = set(more), set()
+        for keys, w in ((reads, False), (writes, True)):
+            for x in keys:
+                for y, yw, i in log.get(x[0], []):
+                    if meet(x, y) and (w or yw or (x[0][:2] == "ps" and nodes[i]["q"] != q)):
+                        (follow if q == "t" and nodes[i]["q"] == "t" else need).add(i)
+        if q in ("g", "y", "v"):
+            if q in tail:
+                follow.add(tail[q])
+            tail[q] = len(nodes)
+        nodes.append({"q": q, "cost": cost, "lag": lag, "need": need, "follow": follow, "call": call, "tok": None})
+        if move:
+            chain = {tail["e"]} if q == "g" and "e" in tail else set()
+            if q == "g":
+                tail["e"] = len(nodes)
+            nodes.append({"q": "e", "cost": move, "lag": lag, "need": {len(nodes) - 1}, "follow": chain, "call": None, "tok": None})
+        for keys, w in ((reads, False), (writes, True)):
+            for x in keys:
+                log.setdefault(x[0], []).append((x, w, len(nodes) - 1))
+        return len(nodes) - 1
+
+    def issue():
+        far = [0.0] * len(nodes)
+        for i in range(len(nodes) - 1, -1, -1):
+            x = nodes[i]
+            far[i] += x["cost"]
+            for j in x["need"]:
+                far[j] = max(far[j], far[i] + nodes[j]["lag"])
+            for j in x["follow"]:
+                far[j] = max(far[j], far[i])
+        busy, start = {}, {}
+        for i in sorted(range(len(nodes)), key=lambda i: (-far[i], i)):
+            x = nodes[i]
+            t = max([0.0] + [start[j] + nodes[j]["cost"] + nodes[j]["lag"] for j in x["need"]]
+                    + [start[j] + nodes[j]["cost"] for j in x["follow"]])
+            if x["q"] != "r":
+                slots = busy.setdefault(x["q"], [])
+                for a, b in slots:
+                    if t + x["cost"] <= a:
+                        break
+                    t = max(t, b)
+                slots.append((t, t + x["cost"]))
+                slots.sort()
+            start[i] = t
+        for i in sorted(range(len(nodes)), key=lambda i: (start[i], i)):
+            x = nodes[i]
+            if x["q"] in ("r", "e"):
+                continue
+            need = {}
+            for j in x["need"]:
+                s, n = nodes[j]["tok"]
+                need[s] = max(need.get(s, 0), n)
+            for s in sorted(need):
+                wait(x["q"], (s, need[s]))
+            x["tok"] = x["call"]()
+            if i + 1 < len(nodes) and nodes[i + 1]["q"] == "e":
+                nodes[i + 1]["tok"] = x["tok"]
+        for s in count:
+            wait("g", (s, count[s]))
+
+    def split(outs, ins):
+        reads, writes = [], []
+        for x in outs:
+            writes += x[1]
+            if len(x) > 2:
+                reads += x[2]
+        for x in ins:
+            if isinstance(x, tuple):
+                reads += x[1]
+                if len(x) > 2:
+                    reads += x[2]
+        return reads, writes
+
+    def ap(x):
+        return x[0] if isinstance(x, tuple) else x
+
+    def size(x):
+        return x[1][0][5]
+
+    def narrow(x):
+        return SCRATCH[x[1][0][0]][2] == BF
+
+    def run(q, outs, ins, call, per=1.0):
+        reads, writes = split(outs, ins)
+        if len(outs[0]) > 2:
+            cost = 50 + SCATTER * size(ins[0])
+        elif ins and len(ins[0]) > 2:
+            cost = 55 + GATHER * size(outs[0])
+        elif q == "v":
+            cost = max(66.0, per * size(outs[0]) * (0.52 if per == 1.0 and narrow(outs[0]) and all(narrow(x) for x in ins[:1]) else 1.04))
+        else:
+            cost = {"s": 66, "g": 130, "t": 10}[q] + per * size(outs[0]) * 1.04
+
+        def go():
+            s = "q" + q
+            count[s] = count.get(s, 0) + 1
+            call().then_inc(T.sem[s], 1)
+            return s, count[s]
+        node(q, reads, writes, cost, WAKE, go)
+
+    def dma(q, out, in_, behind=()):
+        reads, writes = split([out], [in_] + list(behind))
+        s = "d%d" % ndma[0]
+        ndma[0] += 1
+
+        def go():
+            count[s] = 16
+            Q[q].dma_start(out[0], in_[0]).then_inc(T.sem[s], 16)
+            return s, 16
+        x = out if out[1] else in_
+        rows = 128 if not x[1][0][4] or x[1][0][4][2] > 1 else 16
+        width = size(x) * BYTES[SCRATCH[x[1][0][0]][2]] * (len(range(*x[1][0][4])) if x[1][0][4] else 128)
+        node(q, reads, writes, 60.0, LOCAL / 2, go, (), (rows * ROW + width / RATE) / 16)
+
+    def cp(out, in_):
+        run("v", [out], [in_], lambda: g.vector.tensor_copy(out[0], in_[0]))
+
+    def tt(out, a, b, op):
+        run("v", [out], [a, b], lambda: g.vector.tensor_tensor(out[0], a[0], b[0], op), 1.0 if a[1][0][0][:2] == "ps" else 2.0)
+
+    def ts(out, a, s1, op0, s2=None, op1=None):
+        if op1 is None:
+            run("v", [out], [a, s1], lambda: g.vector.tensor_scalar(out[0], a[0], ap(s1), None, op0))
+        else:
+            run("v", [out], [a, s1, s2], lambda: g.vector.tensor_scalar(out[0], a[0], ap(s1), ap(s2), op0, op1))
+
+    def scan(out, d0, d1, init, op0, op1):
+        run("v", [out], [d0, d1, init], lambda: g.vector.tensor_tensor_scan(out[0], d0[0], d1[0], ap(init), op0, op1))
+
+    def tr(out, in_):
+        run("v", [out], [in_], lambda: g.vector.transpose(out[0], in_[0]))
+
+    def fill(out, c):
+        run("v", [out], [], lambda: g.vector.memset(out[0], c))
+
+    def act(out, in_, scale=None):
+        if scale is None:
+            run("s", [out], [in_], lambda: g.scalar.activation(out[0], in_[0], COPY))
+        else:
+            run("s", [out], [in_], lambda: g.scalar.activation(out[0], in_[0], COPY, scale=scale))
+
+    def sfill(name, n, c):
+        for a in range(0, n, 512):
+            o, z = R(name, a, min(n, a + 512)), R("zb", 0, min(n - a, 512))
+            run("s", [o], [z], lambda o=o, z=z: g.scalar.activation(o[0], z[0], IDENT, bias=c))
+
+    def iota(out, pattern, base, cm, real=False):
+        if real:
+            run("g", [out], [], lambda: g.iota(out[0], pattern, base, cm, allow_small_or_imprecise_dtypes=True), 2.0)
+        else:
+            run("g", [out], [], lambda: g.iota(out[0], pattern, base, cm), 2.0)
+
+    def quant(name, a, n, tile):
+        q, z = R(name + "q", a, a + n), R(name + "z", a, a + n)
+        run("v", [q, z], [tile], lambda: g.vector.quantize_mx(q[0], z[0], tile[0]), 1.1)
+
+    def mm(bank, wn, wa, xn, xa, n, start, stop):
+        o = R("ps%d" % bank, 0, n)
+        i = [R(wn + "q", wa, wa + 128), R(wn + "z", wa, wa + 128), R(xn + "q", xa, xa + n), R(xn + "z", xa, xa + n)]
+        run("t", [o], i, lambda: g.tensor.matmul_mx(o[0], i[0][0], i[1][0], i[2][0], i[3][0], start, stop), 0.6)
+
+    def bits(e):
+        return sum(1 << x for x in e)
+
+    def dst(x):
+        rid, pid, se = topo.addr(cores[x])
+        return DstId(rid=rid, pnc=pid)
+
+    def send(sem, items):
+        reads = []
+        for x in items:
+            reads += x[0][1]
+        width = size(items[0][0]) * BYTES[SCRATCH[reads[0][0]][2]]
+        cost = sum(len(x[1]) for x in items) * 128 * (ROW + width / RATE) / 14
+
+        def go():
+            moves = [RemoteDMATransfer(dst_ids=[dst(a) for a, d in to], dma_engine_mask=bits(e), remote_sem=T.sem["in_" + sem],
+                                       srcs=[src[0]], dsts=[d[0] for a, d in to]) for src, to, e in items]
+            g.remote_dma_fused(moves, local_sem=T.sem.sent)
+            count["sent"] = count.get("sent", 0) + sum(len(x[2]) for x in items)
+        cost0 = 300.0 + (0 if sent else FIRST)
+        sent.setdefault(sem, []).append(node("g", reads, [], cost0, REMOTE / 2, go, (), cost))
+
+    def lands(sem, name, ranges, n):
+        count["in_" + sem] = n
+        i = node("r", [], [(name, a, b, 1, None, b - a) for a, b in ranges], 1.0, 0.0, None, sent[sem])
+        nodes[i]["tok"] = ("in_" + sem, n)
+
+    def share(e, n):
+        k = 1
+        while 2 * k * n <= len(e):
+            k *= 2
+        return [e[k * i:k * i + k] for i in range(n)]
+
+    def spread_codes(name):
+        x = u8(R(name + "q", C * r, C * r + C))
+        send(name + "q", [(x, [(a, x) for a in others[:nx]], even), (x, [(a, x) for a in others[nx:]], odd)])
+        lands(name + "q", name + "q", [(C * a, C * a + C) for a in others], len(even) * (N - 1))
+
+    def spread_scales(name):
+        x = R(name + "z", C * r, C * r + C)
+        send(name + "z", [(x, [(a, x) for a in others[:nx // 2]], even), (x, [(a, x) for a in others[nx // 2:]], odd)])
+        lands(name + "z", name + "z", [(C * a, C * a + C) for a in others], len(even) * (N - 1))
+
+    def place(a):
+        return order(a).index(r)
+
+    top = {"rf": 0, "ri": 0, "ru": 0, "cf": 0, "ci": 0, "cu": 0}
+
+    def new(name, n):
+        o = top[name]
+        top[name] = o + (n + 31) // 32 * 32
+        return lambda a=0, b=n, s=1: R(name, o + a, o + b, s)
+
+    pcol = new("ci", 4)
+    iota(pcol(0, 1), [[0, 1]], 0, 1)
+    iota(R("flat"), [[1, 16], [0, 2], [16, 16]], C * r, 0)
+    iota(R("idt"), [[-1, 128]], 0, 1, True)
+    dma("y", R("jn"), ext(T.jb[:]))
+    dma("s", R("xct"), ext(T.xc[:]))
+    dma("y", R("flat", 0, 512, 1, (0, 128, 16)), ext(T.jb[:]))
+    dma("y", R("flat", 0, 512, 1, (1, 128, 16)), ext(T.kc[:]))
+    dma("y", R("xbt"), ext(T.xb[:]))
+    dma("y", R("kn"), ext(T.kc[:]))
+    dma("y", R("vt"), ext(T.v[:]))
+    dma("y", u8(R("wq")), ext(T.wc[:]))
+    dma("y", R("wz"), ext(T.ws[:]))
+    W7 = 32 * (N - 1)
+    r16, r7, zero, col = new("cf", W7), new("cf", W7), new("cf", 16), new("cf", 8)
+    fill(R("zb"), 0.0)
+    fill(r16(), 1.0)
+    fill(r7(), 1.0)
+    ts(pcol(1, 2), pcol(0, 1), 31, A.bitwise_and)
+    ts(pcol(2, 3), pcol(0, 1), 16, A.bitwise_and)
+    ts(pcol(3, 4), pcol(0, 1), 15, A.bitwise_and)
+    fill(zero(), 0.0)
+    fill(r16(0, W7, 16), 0.0)
+    fill(r7(0, W7, N - 1), 0.0)
+    m0, m1, g16, base, own0, own1, p32, pk = [col(k, k + 1) for k in range(8)]
+    ts(m0, pcol(2, 3), 0.0, A.is_equal)
+    ts(m1, pcol(2, 3), 16.0, A.is_equal)
+    cp(g16, pcol(2, 3))
+    cp(p32, pcol(1, 2))
+    ts(base, pcol(1, 2), float(S), A.mult, -1.0, A.add)
+    ts(own0, pcol(2, 3), -1.0, A.mult, float(WQ), A.add)
+    ts(own1, pcol(2, 3), -1.0, A.mult, float(WQ + 16), A.add)
+    ts(pk, pcol(3, 4), float(K), A.mult)
+    sfill("win0", WQ, PAD)
+    sfill("eb", 4 * 516, 0.0)
+    sfill("fr0", L, 0.0)
+    sfill("win1", L, PAD)
+
+    def ready():
+        tot, u = new("rf", 32), new("rf", 32)
+        fill(tot(), 0.0)
+        cp(u(0, 1), base)
+        cp(u(16, 17), base)
+        return tot, u
+
+    def route(jo, pre, vals, k):
+        tot, u = pre
+        o, x, hi, pi, t, t2 = [new("ri", 32) for i in range(6)]
+        h, s1, h2, s2, w, w2 = [new("rf", W7) for i in range(6)]
+        ho, a1, a2, a3, a4, a5, tt_, ut, uu, ad = [new("rf", 32) for i in range(10)]
+        off = new("ru", 32)
+        ts(o(), jo, 8, A.arith_shift_right)
+        ts(x(), jo, C - 1, A.bitwise_and)
+        for i, a in enumerate(others):
+            ts(h(32 * i, 32 * i + 32), o(), float(a), A.is_equal)
+        ts(hi(), x(), 4, A.arith_shift_right)
+        scan(s1(), r16(), h(), 0.0, A.mult, A.add)
+        ts(ho(), o(), float(r), A.is_equal)
+        cp(tot(0, 2 * N - 2), s1(15, W7, 16))
+        ts(a1(0, 16), x(0, 16), 32.0, A.mult, own0 if k == 0 else float(WQ), A.add)
+        tr(tt_(), tot())
+        ts(a1(16, 32), x(16, 32), 32.0, A.mult, own1 if k == 0 else float(WQ + 16), A.add)
+        scan(u(1, 16), tt_(0, 15), zero(0, 15), base, A.add, A.add)
+        scan(u(17, 32), tt_(16, 31), zero(0, 15), base, A.add, A.add)
+        cp(h2(), h())
+        tr(ut(), u())
+        ts(a2(), hi(), -511.0, A.mult)
+        tt(h2(0, W7, 16), h(0, W7, 16), ut(0, 2 * N - 2), A.add)
+        tt(a3(), a1(), a2(), A.add)
+        scan(s2(), r16(), h2(), 0.0, A.mult, A.add)
+        tt(a4(), a3(), ho(), A.mult)
+        for i in range(N - 1):
+            tt(w(i, W7, N - 1), s2(32 * i, 32 * i + 32), h(32 * i, 32 * i + 32), A.mult)
+        scan(w2(), r7(), w(), 0.0, A.mult, A.add)
+        p = w2(N - 2, W7, N - 1)
+        cp(pi(), p)
+        if k == 1:
+            ts(t(), pi(), 15, A.bitwise_and)
+            ts(t2(), pi(), 4, A.arith_shift_right)
+            ts(a5(), t(), float(K), A.mult)
+            tt(uu(), t2(), a4(), A.add)
+            tt(ad(), a5(), uu(), A.add)
+            cp(off(0, 32, 2), ad(0, 16))
+            cp(off(1, 32, 2), ad(16, 32))
+        else:
+            tt(uu(), p, a4(), A.add)
+            ts(t(), pi(), 0x7FF0, A.bitwise_and)
+            tt(ad(), t(), uu(), A.add)
+            ts(off(0, 32, 2), ad(0, 16), g16, A.add)
+            ts(off(1, 32, 2), ad(16, 32), g16, A.add)
+        cp(ind(R("win%d" % k, 0, WQ + 512), off()), vals)
+        return p, x, ho
+
+    def ask(k, n, sem, i0, i1):
+        e = share(eng, i1 - i0)
+        send(sem, [(R("rq%d" % k, n * i, n * i + n), [(others[i], R("rl%d" % k, n * place(others[i]), n * place(others[i]) + n))], e[i - i0])
+                   for i in range(i0, i1)])
+        lands(sem, "rl%d" % k, [(n * i0, n * i1)], len(e[0]) * (i1 - i0))
+
+    def unwrap(k, rows):
+        for l, j in rows:
+            x = new("rf", K)
+            cp(x(), R("rl%d" % k, l, (3 - k) * K, 3 - k))
+            dma("y", R("fr%d" % k, 0, L, 1, (j, 128, 16)), x())
+
+    todo = {}
+
+    def invert(k):
+        act(R("fl%d" % k), ind(R("fr%d" % k), turn()))
+        x, hi = new("ri", K), new("ri", K)
+        a1, a2, mk, md, a3, a4, a5 = [new("rf", K) for i in range(7)]
+        off = new("ru", K)
+        rl = R("rl%d" % k, 0, (3 - k) * K, 3 - k)
+        ts(x(), rl, float(C * r), A.subtract, float(C - 1), A.min)
+        ts(mk(), rl, float(N * C), A.is_ge)
+        ts(hi(), x(), 4, A.arith_shift_right)
+        ts(a1(), x(), 32.0, A.mult)
+        tt(md(), mk(), behind(), A.mult)
+        ts(a2(), hi(), -511.0, A.mult)
+        tt(a4(), md(), half16(), A.add)
+        tt(a3(), a1(), a2(), A.add)
+        tt(a5(), a3(), a4(), A.add)
+        cp(off(), a5())
+        todo[k] = lambda: cp(ind(R("win%d" % k, WQ, WIN), off()), R("fl%d" % k))
+
+    def lists(src, adds, move):
+        n = 64 * len(adds)
+        z, d, u = new("rf", n), new("rf", n), new("ru", n)
+        for l in range(len(adds)):
+            for y in range(2):
+                for e in range(2):
+                    a = 64 * l + 32 * y + 16 * e
+                    move(z(a, a + 16), src(l, y))
+        tr(d(), z())
+        for l, c in enumerate(adds):
+            ts(u(64 * l, 64 * l + 64), d(64 * l, 64 * l + 64), float(c), A.add)
+        return d, [(lambda y, h, n=16, l=l: u(64 * l + 32 * y + 16 * h, 64 * l + 32 * y + 16 * h + n)) for l in range(len(adds))]
+
+    def table(k, rows, adds, move):
+        t1 = new("rf", 512)
+        tr(t1(), R("win%d" % k, WQ, WQ + 512))
+        return lambda: lists(lambda l, y: t1(16 * y + rows[l], 512, 32), adds, move)
+
+    def pick(dn, a, n, sn, off):
+        w = T[sn + "q"].shape[1]
+        cp(u32(R(dn + "q", a, a + n)), ind(u32(R(sn + "q", 0, w)), off))
+        act(R(dn + "z", a, a + n), ind(R(sn + "z", 0, w), off))
+
+    def early(mode, sn, off):
+        dn = "p%d" % (2 * mode)
+        for y in range(2):
+            pick(dn, 512 * y, 512, sn, off(y, 0, 32))
+            for b in range(4):
+                mm(b, "e", 128 * (4 * y + b), dn, 512 * y, 512, y == 0, y == 1)
+        for b in range(4):
+            act(R("gs%d" % mode, 512 * b, 512 * b + 512), R("ps%d" % b, 0, 512))
+
+    def make(mode, sn, off, done, other=None, middle=None):
+        dn, gs, mn, nt = "p%d" % (2 * mode + 1), "gs%d" % mode, "m%d" % mode, "nt%d" % mode
+
+        def unpack(dn, sn, off, h, bank):
+            for y in range(2):
+                pick(dn, 512 * y + 256 * h, 256, sn, off(y, h))
+                for b in range(4):
+                    mm(bank + b, "e", 128 * (4 * y + b), dn, 512 * y + 256 * h, 256, y == 0, y == 1)
+
+        def times(h, bank):
+            for b in range(4):
+                tt(R("pr", 1024 * h + b, 1024 * h + 1024, 4), R("ps%d" % (bank + b), 0, 256),
+                   R(gs, 512 * b + 256 * h, 512 * b + 256 * h + 256), A.mult)
+
+        if other:
+            for h in range(2):
+                unpack("p%d" % (2 * mode), other[0], other[1], h, 0)
+                for b in range(4):
+                    act(R(gs, 512 * b + 256 * h, 512 * b + 256 * h + 256), R("ps%d" % b, 0, 256))
+        unpack(dn, sn, off, 0, 4)
+        unpack(dn, sn, off, 1, 0)
+        times(0, 4)
+        if middle:
+            middle()
+        times(1, 0)
+        for X in range(2):
+            a = 512 * X
+            tt(R("mt", a, a + 512), R("pr", a, a + 512), R("pr", 1024 + a, 1536 + a), A.add)
+            quant(mn, 128 * X, 128, R("mt", a, a + 512))
+            for b in range(4):
+                mm(4 - 4 * X + b, "w", 128 * b, mn, 128 * X, 128, True, True)
+            if X == 0:
+                for b in range(4):
+                    act(R(nt, b, 512, 4), R("ps%d" % (4 + b), 0, 128), 0.03125)
+        done(0)
+        for b in range(2):
+            ts(R(nt, 512 + b, 1024, 4), R("ps%d" % b, 0, 128), 0.03125, A.mult)
+            act(R(nt, 514 + b, 1024, 4), R("ps%d" % (2 + b), 0, 128), 0.03125)
+        done(1)
+
+    def compose(k, win, off, land, ahead, meanwhile):
+        ct, tn = "ct%d" % k, "t%d" % k
+        ec = [share(even, nx), share(eng, N - 1 - nx)]
+        ez = [share(odd, nx), share(eng[::-1], N - 1 - nx)]
+        for c, (i0, i1) in enumerate(((0, nx), (nx, N - 1))):
+            ahead(c, i0, i1)
+            for t in range(4):
+                (cp if t < 2 - c else act)(R(ct, 4 * B * i0 + t, 4 * B * i1, 4), ind(win(t), off(t, 6 * i0, 6 * i1)))
+                meanwhile.get((c, t), lambda: None)()
+            quant(tn, B * i0, B * (i1 - i0), R(ct, 4 * B * i0, 4 * B * i1))
+            for z, e, f in (("q", ec[c], u8), ("z", ez[c], lambda x: x)):
+                send(land + z, [(f(R(tn + z, B * i, B * i + B)),
+                                 [(others[i], f(R(land + z, B * place(others[i]), B * place(others[i]) + B)))], e[i - i0])
+                                for i in range(i0, i1)])
+        for z, e in (("q", ec), ("z", ez)):
+            lands(land + z, land + z, [(0, L)], nx * len(e[0][0]) + (N - 1 - nx) * len(e[1][0]))
+
+    def codes_out(f, name, at):
+        dma("y", ext(T.oc[:, 4 * C * f:4 * C * f + 4 * C]), u8(R(name + "q", at, at + C)), [R(name + "q"), R(name + "z")])
+        for k in range(4):
+            dma("y", ext(T.osc[4 * k:4 * k + 4, C * f:C * f + C]), R(name + "z", at, at + C, 1, (32 * k, 32 * k + 4, 1)))
+
+    def y_part(bank, f, name, at, a, n):
+        mm(bank, "v", 0, name, at + a, n, True, True)
+        act(R("ysb", C * f + a, C * f + a + n), R("ps%d" % bank, 0, n))
+
+    def y_out(f, q):
+        dma(q, ext(T.y[:, C * f:C * f + C]), R("ysb", C * f, C * f + C))
+
+    pre0 = ready()
+    xj, xt, jo = new("rf", 64), new("rf", 64), new("ri", 32)
+    for h in range(2):
+        ts(xj(32 * h, 32 * h + 16), R("jn", 16 * h, 16 * h + 16), m0, A.mult)
+        ts(xj(32 * h + 16, 32 * h + 32), R("jn", 16 * h, 16 * h + 16), m1, A.mult)
+    tr(xt(), xj())
+    for h in range(2):
+        tt(jo(16 * h, 16 * h + 16), xt(32 * h, 32 * h + 16), xt(32 * h + 16, 32 * h + 32), A.add)
+    quant("c0", C * r, C, R("xct"))
+    spread_codes("c0")
+    c32, c1, half16, behind, turn = new("ci", K), new("ci", K), new("cf", K), new("cf", K), new("cu", K)
+    iota(c32(), [[32, K]], 0, 0)
+    iota(c1(), [[1, K]], 0, 0)
+    iota(half16(), [[0, N - 1], [16, 2], [0, 3]], 0, 0, True)
+    p, x, ho = route(jo(), pre0, R("flat"), 0)
+    for sem, i0, i1 in (("far0", 0, nx), ("near0", nx, N - 1)):
+        a, b = 2 * B * i0, 2 * B * i1
+        tr(R("wt0", a, b), R("win0", a, b))
+        for l, j in enumerate((0, 1, 9)):
+            tt(R("rq0", 18 * i0 + l, 18 * i1, 3), R("wt0", a + j, b, 32), R("wt0", a + 16 + j, b, 32), A.min)
+        ask(0, 18, sem, i0, i1)
+    spread_scales("c0")
+    iota(R("fr1"), [[1, 16], [16, K]], C * r - L, 0, True)
+    for t in range(4):
+        act(R("xbp", C * t, C * t + C), R("xbt", t, 4 * C, 4))
+    ts(turn(), c1(), pk, A.add)
+    ts(behind(), c32(), p32, A.add, 32.0, A.add)
+
+    po, pa, z, d, u = new("rf", 32), new("rf", 32), new("rf", 64), new("rf", 64), new("ru", 64)
+    kf, kt = new("rf", 32), new("rf", 32)
+    ts(po(), x(), float(L), A.add)
+    cp(kf(), R("kn"))
+    tt(po(), po(), ho(), A.mult)
+    tr(kt(), kf())
+    tt(pa(), po(), p, A.add)
+    offc0 = lists(lambda l, y: kt(16 * y, 16 * y + 16), [0], cp)[1][0]
+    for h in range(2):
+        for e in range(2):
+            cp(z(32 * h + 16 * e, 32 * h + 16 * e + 16), pa(16 * h, 16 * h + 16))
+    tr(d(), z())
+    for y, m in enumerate((m0, m1)):
+        for e in range(2):
+            a = 516 * (2 * y + e)
+            ts(R("eb", a + 2 + e, a + 514, 4), R("idt"), 0.0, A.is_equal, m, A.mult)
+    cp(u(), d())
+    offb0 = lambda y, h: u(32 * h + 16 * y, 32 * h + 16 * y + 16)
+    for y in range(2):
+        for b in range(4):
+            a = 516 * (2 * y + b % 2) + (2 if b < 2 else 0)
+            quant("e", 128 * (4 * y + b), 128, R("eb", a, a + 512))
+
+    og = new("ru", K)
+
+    def wanted(c, i0, i1):
+        ts(og(6 * i0, 6 * i1), R("rl0", 18 * i0, 18 * i1, 3), float(C * r), A.subtract, float(C - 1), A.min)
+
+    compose(0, lambda t: R("xbp", C * t, C * t + C), lambda t, a, b: og(a, b), "b0", wanted,
+            {(0, 1): lambda: unwrap(0, ((0, 0), (1, 1), (2, 9))), (1, 0): lambda: (quant("b0", L, C, R("xbt")), invert(0))})
+    early(0, "c0", offc0)
+    todo[0]()
+    rest = table(0, (9, 1), (0, 0), act)
+
+    make(0, "b0", offb0, lambda X: quant("a", C * r + 128 * X, 128, R("nt0", 512 * X, 512 * X + 512)))
+    spread_codes("a")
+    spread_scales("a")
+    d2, (offa1, offc1) = rest()
+
+    pre1 = ready()
+    xk, xu, ko = new("rf", 64), new("rf", 64), new("ri", 32)
+    for h in range(2):
+        for y in range(2):
+            act(xk(32 * h + 16 * y, 32 * h + 16 * y + 16), d2(64 + 32 * y + 16 * h, 64 + 32 * y + 16 * h + 16))
+    early(1, "c0", offc1)
+    tr(xu(), xk())
+    for h in range(2):
+        cp(ko(16 * h, 16 * h + 16), xu(32 * h, 32 * h + 16))
+    route(ko(), pre1, R("win0", WQ, WQ + 512), 1)
+    kw, jw, jl, o4 = new("rf", 2 * K), new("rf", K), new("rf", K), [new("ru", K) for t in range(4)]
+    for j, to in ((1, kw(0, K)), (9, kw(K, 2 * K)), (0, jw())):
+        dma("y", to, R("win1", 0, L, 1, (j, 128, 16)))
+    codes_out(0, "a", C * r)
+
+    def ask_k():
+        cp(R("rq1", 0, 2 * K, 2), kw(0, K))
+        cp(R("rq1", 1, 2 * K, 2), kw(K, 2 * K))
+        ask(1, 12, "all1", 0, N - 1)
+        ts(jl(), jw(), float(C * r), A.subtract, float(C - 1), A.min)
+        for t in range(4):
+            ts(o4[t](), jl(), 4.0, A.mult, float(t), A.add)
+
+    make(1, "a", offa1, lambda X: None, None, ask_k)
+    compose(1, lambda t: R("nt1"), lambda t, a, b: o4[t](a, b), "b1", lambda c, i0, i1: None,
+            {(0, 0): lambda: unwrap(1, ((1, 9),)), (1, 0): lambda: quant("b1", L, C, R("nt1"))})
+    quant("v", 0, 128, R("vt"))
+    y_part(7, 0, "a", C * r, 0, C)
+    y_part(6, 1, "b1", L, 0, C)
+    invert(1)
+    todo[1]()
+    offb2, offa2 = table(1, (0, 9), (L - C * r, 0), cp)()[1]
+    codes_out(1, "b1", L)
+    dma("y", ext(T.y[:, 0:2 * C]), R("ysb", 0, 2 * C))
+
+    def last(X):
+        quant("c1", 128 * X, 128, R("nt2", 512 * X, 512 * X + 512))
+        y_part(5 + X, 2, "c1", 0, 128 * X, 128)
+
+    make(2, "b1", offb2, last, ("a", offa2))
+    codes_out(2, "c1", 0)
+    y_out(2, "s")
+
+    issue()

@@ -32,7 +32,7 @@ for _n, _w in (("w", 512), ("v", 128), ("e", 1024), ("c0", N * C), ("a", N * C),
     _sb(_n + "q", _w, X4)
     _sb(_n + "z", _w, U8)
 _sb("idt", 128, F32)
-_sb("cf", 768, F32)
+_sb("cf", 896, F32)
 _sb("ci", 192, I32)
 _sb("cu", 64, U16)
 _sb("rf", 7168, F32)
@@ -53,7 +53,7 @@ SEMAPHORES = ["qv", "qs", "qt", "qg", "sent"] + ["in_" + x for x in ARR] + ["d%d
 A = AluOpType
 COPY = ActivationFunctionType.Copy
 IDENT = ActivationFunctionType.Identity
-WAKE, LOCAL, REMOTE, FIRST, ROW, RATE, GATHER, SCATTER = 70.0, 2000.0, 2000.0, 3200.0, 25.0, 20.0, 1.62, 3.9
+WAKE, LOCAL, REMOTE, FIRST, ROW, RATE, GATHER, SCATTER = 150.0, 1800.0, 2000.0, 2700.0, 15.0, 35.0, 1.45, 2.8
 
 
 def rank_program(g, core, T, topo):
@@ -140,20 +140,22 @@ def rank_program(g, core, T, topo):
                 far[j] = max(far[j], far[i] + nodes[j]["lag"])
             for j in x["follow"]:
                 far[j] = max(far[j], far[i])
-        busy, start = {}, {}
-        for i in sorted(range(len(nodes)), key=lambda i: (-far[i], i)):
-            x = nodes[i]
-            t = max([0.0] + [start[j] + nodes[j]["cost"] + nodes[j]["lag"] for j in x["need"]]
-                    + [start[j] + nodes[j]["cost"] for j in x["follow"]])
-            if x["q"] != "r":
-                slots = busy.setdefault(x["q"], [])
-                for a, b in slots:
-                    if t + x["cost"] <= a:
-                        break
-                    t = max(t, b)
-                slots.append((t, t + x["cost"]))
-                slots.sort()
-            start[i] = t
+        start = [-x for x in far]
+        for turn in range(2):
+            busy, rank = {}, list(start)
+            for i in sorted(range(len(nodes)), key=lambda i: (rank[i], i)):
+                x = nodes[i]
+                t = max([0.0] + [start[j] + nodes[j]["cost"] + nodes[j]["lag"] for j in x["need"]]
+                        + [start[j] + nodes[j]["cost"] for j in x["follow"] if turn == 0 or x["q"] != "v"])
+                if x["q"] != "r":
+                    slots = busy.setdefault(x["q"], [])
+                    for a, b in slots:
+                        if t + x["cost"] <= a:
+                            break
+                        t = max(t, b)
+                    slots.append((t, t + x["cost"]))
+                    slots.sort()
+                start[i] = t
         for i in sorted(range(len(nodes)), key=lambda i: (start[i], i)):
             x = nodes[i]
             if x["q"] in ("r", "e"):
@@ -249,7 +251,8 @@ def rank_program(g, core, T, topo):
         if scale is None:
             run("s", [out], [in_], lambda: g.scalar.activation(out[0], in_[0], COPY))
         else:
-            run("s", [out], [in_], lambda: g.scalar.activation(out[0], in_[0], COPY, scale=scale))
+            f = IDENT if isinstance(scale, tuple) else COPY
+            run("s", [out], [in_, scale], lambda: g.scalar.activation(out[0], in_[0], f, scale=ap(scale)))
 
     def sfill(name, n, c):
         for a in range(0, n, 512):
@@ -326,8 +329,8 @@ def rank_program(g, core, T, topo):
 
     pcol = new("ci", 4)
     iota(pcol(0, 1), [[0, 1]], 0, 1)
-    iota(R("flat"), [[1, 16], [0, 2], [16, 16]], C * r, 0)
     iota(R("idt"), [[-1, 128]], 0, 1, True)
+    iota(R("flat"), [[1, 16], [0, 2], [16, 16]], C * r, 0)
     dma("y", R("jn"), ext(T.jb[:]))
     dma("s", R("xct"), ext(T.xc[:]))
     dma("y", R("flat", 0, 512, 1, (0, 128, 16)), ext(T.jb[:]))
@@ -357,6 +360,7 @@ def rank_program(g, core, T, topo):
     ts(own0, pcol(2, 3), -1.0, A.mult, float(WQ), A.add)
     ts(own1, pcol(2, 3), -1.0, A.mult, float(WQ + 16), A.add)
     ts(pk, pcol(3, 4), float(K), A.mult)
+    ident = new("cf", 128)
     sfill("win0", WQ, PAD)
     sfill("eb", 4 * 516, 0.0)
     sfill("fr0", L, 0.0)
@@ -498,9 +502,11 @@ def rank_program(g, core, T, topo):
         if other:
             for h in range(2):
                 unpack("p%d" % (2 * mode), other[0], other[1], h, 0)
-                for b in range(4):
+                for b in range(2 * h, 4):
                     act(R(gs, 512 * b + 256 * h, 512 * b + 256 * h + 256), R("ps%d" % b, 0, 256))
         unpack(dn, sn, off, 0, 4)
+        for b in range(2 if other else 0):
+            cp(R(gs, 512 * b + 256, 512 * b + 512), R("ps%d" % b, 0, 256))
         unpack(dn, sn, off, 1, 0)
         times(0, 4)
         if middle:
@@ -528,7 +534,7 @@ def rank_program(g, core, T, topo):
         for c, (i0, i1) in enumerate(((0, nx), (nx, N - 1))):
             ahead(c, i0, i1)
             for t in range(4):
-                (cp if t < 2 - c else act)(R(ct, 4 * B * i0 + t, 4 * B * i1, 4), ind(win(t), off(t, 6 * i0, 6 * i1)))
+                (cp if t < 2 else act)(R(ct, 4 * B * i0 + t, 4 * B * i1, 4), ind(win(t), off(t, 6 * i0, 6 * i1)))
                 meanwhile.get((c, t), lambda: None)()
             quant(tn, B * i0, B * (i1 - i0), R(ct, 4 * B * i0, 4 * B * i1))
             for z, e, f in (("q", ec[c], u8), ("z", ez[c], lambda x: x)):
@@ -551,6 +557,7 @@ def rank_program(g, core, T, topo):
         dma(q, ext(T.y[:, C * f:C * f + C]), R("ysb", C * f, C * f + C))
 
     pre0 = ready()
+    ts(ident(), R("idt"), 0.0, A.is_equal)
     xj, xt, jo = new("rf", 64), new("rf", 64), new("ri", 32)
     for h in range(2):
         ts(xj(32 * h, 32 * h + 16), R("jn", 16 * h, 16 * h + 16), m0, A.mult)
@@ -560,6 +567,7 @@ def rank_program(g, core, T, topo):
         tt(jo(16 * h, 16 * h + 16), xt(32 * h, 32 * h + 16), xt(32 * h + 16, 32 * h + 32), A.add)
     quant("c0", C * r, C, R("xct"))
     spread_codes("c0")
+    spread_scales("c0")
     c32, c1, half16, behind, turn = new("ci", K), new("ci", K), new("cf", K), new("cf", K), new("cu", K)
     iota(c32(), [[32, K]], 0, 0)
     iota(c1(), [[1, K]], 0, 0)
@@ -571,7 +579,6 @@ def rank_program(g, core, T, topo):
         for l, j in enumerate((0, 1, 9)):
             tt(R("rq0", 18 * i0 + l, 18 * i1, 3), R("wt0", a + j, b, 32), R("wt0", a + 16 + j, b, 32), A.min)
         ask(0, 18, sem, i0, i1)
-    spread_scales("c0")
     iota(R("fr1"), [[1, 16], [16, K]], C * r - L, 0, True)
     for t in range(4):
         act(R("xbp", C * t, C * t + C), R("xbt", t, 4 * C, 4))
@@ -585,15 +592,15 @@ def rank_program(g, core, T, topo):
     tt(po(), po(), ho(), A.mult)
     tr(kt(), kf())
     tt(pa(), po(), p, A.add)
-    offc0 = lists(lambda l, y: kt(16 * y, 16 * y + 16), [0], cp)[1][0]
+    offc0 = lists(lambda l, y: kt(16 * y, 16 * y + 16), [0], act)[1][0]
     for h in range(2):
         for e in range(2):
-            cp(z(32 * h + 16 * e, 32 * h + 16 * e + 16), pa(16 * h, 16 * h + 16))
+            act(z(32 * h + 16 * e, 32 * h + 16 * e + 16), pa(16 * h, 16 * h + 16))
     tr(d(), z())
     for y, m in enumerate((m0, m1)):
         for e in range(2):
             a = 516 * (2 * y + e)
-            ts(R("eb", a + 2 + e, a + 514, 4), R("idt"), 0.0, A.is_equal, m, A.mult)
+            act(R("eb", a + 2 + e, a + 514, 4), ident(), m)
     cp(u(), d())
     offb0 = lambda y, h: u(32 * h + 16 * y, 32 * h + 16 * y + 16)
     for y in range(2):
@@ -607,7 +614,8 @@ def rank_program(g, core, T, topo):
         ts(og(6 * i0, 6 * i1), R("rl0", 18 * i0, 18 * i1, 3), float(C * r), A.subtract, float(C - 1), A.min)
 
     compose(0, lambda t: R("xbp", C * t, C * t + C), lambda t, a, b: og(a, b), "b0", wanted,
-            {(0, 1): lambda: unwrap(0, ((0, 0), (1, 1), (2, 9))), (1, 0): lambda: (quant("b0", L, C, R("xbt")), invert(0))})
+            {(0, 1): lambda: unwrap(0, ((0, 0), (1, 1), (2, 9))),
+             (1, 0): lambda: (quant("b0", L, C, R("xbt")), invert(0), quant("v", 0, 128, R("vt")))})
     early(0, "c0", offc0)
     todo[0]()
     rest = table(0, (9, 1), (0, 0), act)
@@ -642,11 +650,10 @@ def rank_program(g, core, T, topo):
 
     make(1, "a", offa1, lambda X: None, None, ask_k)
     compose(1, lambda t: R("nt1"), lambda t, a, b: o4[t](a, b), "b1", lambda c, i0, i1: None,
-            {(0, 0): lambda: unwrap(1, ((1, 9),)), (1, 0): lambda: quant("b1", L, C, R("nt1"))})
-    quant("v", 0, 128, R("vt"))
+            {(0, 0): lambda: unwrap(1, ((1, 9),)), (1, 0): lambda: invert(1)})
+    quant("b1", L, C, R("nt1"))
     y_part(7, 0, "a", C * r, 0, C)
     y_part(6, 1, "b1", L, 0, C)
-    invert(1)
     todo[1]()
     offb2, offa2 = table(1, (0, 9), (L - C * r, 0), cp)()[1]
     codes_out(1, "b1", L)

@@ -53,7 +53,7 @@ SEMAPHORES = ["qv", "qs", "qt", "qg", "sent"] + ["in_" + x for x in ARR] + ["d%d
 A = AluOpType
 COPY = ActivationFunctionType.Copy
 IDENT = ActivationFunctionType.Identity
-WAKE, LOCAL, REMOTE, FIRST, ROW, RATE, GATHER, SCATTER = 150.0, 1800.0, 2000.0, 2700.0, 15.0, 35.0, 1.45, 2.8
+WAKE, LOCAL, REMOTE, FIRST, ROW, RATE, GATHER, SCATTER = 200.0, 1800.0, 2000.0, 2700.0, 15.0, 35.0, 1.45, 2.8
 
 
 def rank_program(g, core, T, topo):
@@ -230,7 +230,8 @@ def rank_program(g, core, T, topo):
         run("v", [out], [in_], lambda: g.vector.tensor_copy(out[0], in_[0]))
 
     def tt(out, a, b, op):
-        run("v", [out], [a, b], lambda: g.vector.tensor_tensor(out[0], a[0], b[0], op), 1.0 if a[1][0][0][:2] == "ps" else 2.0)
+        run("v", [out], [a, b], lambda: g.vector.tensor_tensor(out[0], a[0], b[0], op),
+            1.0 if a[1][0][0][:2] == "ps" else (1.01 if narrow(out) else 2.0))
 
     def ts(out, a, s1, op0, s2=None, op1=None):
         if op1 is None:
@@ -373,7 +374,7 @@ def rank_program(g, core, T, topo):
         cp(u(16, 17), base)
         return tot, u
 
-    def route(jo, pre, vals, k):
+    def route(jo, pre, vals, k, more=lambda: None):
         tot, u = pre
         o, x, hi, pi, t, t2 = [new("ri", 32) for i in range(6)]
         h, s1, h2, s2, w, w2 = [new("rf", W7) for i in range(6)]
@@ -388,28 +389,36 @@ def rank_program(g, core, T, topo):
         ts(ho(), o(), float(r), A.is_equal)
         cp(tot(0, 2 * N - 2), s1(15, W7, 16))
         ts(a1(0, 16), x(0, 16), 32.0, A.mult, own0 if k == 0 else float(WQ), A.add)
+        more()
         tr(tt_(), tot())
+        more()
         ts(a1(16, 32), x(16, 32), 32.0, A.mult, own1 if k == 0 else float(WQ + 16), A.add)
         scan(u(1, 16), tt_(0, 15), zero(0, 15), base, A.add, A.add)
         scan(u(17, 32), tt_(16, 31), zero(0, 15), base, A.add, A.add)
         cp(h2(), h())
         tr(ut(), u())
+        more()
         ts(a2(), hi(), -511.0, A.mult)
         tt(h2(0, W7, 16), h(0, W7, 16), ut(0, 2 * N - 2), A.add)
         tt(a3(), a1(), a2(), A.add)
+        more()
         scan(s2(), r16(), h2(), 0.0, A.mult, A.add)
         tt(a4(), a3(), ho(), A.mult)
+        more()
         for i in range(N - 1):
             tt(w(i, W7, N - 1), s2(32 * i, 32 * i + 32), h(32 * i, 32 * i + 32), A.mult)
         scan(w2(), r7(), w(), 0.0, A.mult, A.add)
         p = w2(N - 2, W7, N - 1)
+        more()
         cp(pi(), p)
+        more()
         if k == 1:
             ts(t(), pi(), 15, A.bitwise_and)
             ts(t2(), pi(), 4, A.arith_shift_right)
             ts(a5(), t(), float(K), A.mult)
             tt(uu(), t2(), a4(), A.add)
             tt(ad(), a5(), uu(), A.add)
+            more()
             cp(off(0, 32, 2), ad(0, 16))
             cp(off(1, 32, 2), ad(16, 32))
         else:
@@ -464,7 +473,7 @@ def rank_program(g, core, T, topo):
         tr(d(), z())
         for l, c in enumerate(adds):
             ts(u(64 * l, 64 * l + 64), d(64 * l, 64 * l + 64), float(c), A.add)
-        return d, [(lambda y, h, n=16, l=l: u(64 * l + 32 * y + 16 * h, 64 * l + 32 * y + 16 * h + n)) for l in range(len(adds))]
+        return d, [(lambda y, h, n=16, l=l: u(64 * l + 32 * y + int(16 * h), 64 * l + 32 * y + int(16 * h) + n)) for l in range(len(adds))]
 
     def table(k, rows, adds, move):
         t1 = new("rf", 512)
@@ -614,8 +623,10 @@ def rank_program(g, core, T, topo):
         ts(og(6 * i0, 6 * i1), R("rl0", 18 * i0, 18 * i1, 3), float(C * r), A.subtract, float(C - 1), A.min)
 
     compose(0, lambda t: R("xbp", C * t, C * t + C), lambda t, a, b: og(a, b), "b0", wanted,
-            {(0, 1): lambda: unwrap(0, ((0, 0), (1, 1), (2, 9))),
-             (1, 0): lambda: (quant("b0", L, C, R("xbt")), invert(0), quant("v", 0, 128, R("vt")))})
+            {(0, 1): lambda: unwrap(0, ((0, 0), (1, 1), (2, 9)))})
+    invert(0)
+    quant("b0", L, C, R("xbt"))
+    quant("v", 0, 128, R("vt"))
     early(0, "c0", offc0)
     todo[0]()
     rest = table(0, (9, 1), (0, 0), act)
@@ -630,11 +641,22 @@ def rank_program(g, core, T, topo):
     for h in range(2):
         for y in range(2):
             act(xk(32 * h + 16 * y, 32 * h + 16 * y + 16), d2(64 + 32 * y + 16 * h, 64 + 32 * y + 16 * h + 16))
-    early(1, "c0", offc1)
+    pieces = [(y, h, X) for y in range(2) for h in range(2) for X in range(2)]
+
+    def piece():
+        y, h, X = pieces.pop(0)
+        pick("p2", 512 * y + 256 * h + 128 * X, 128, "c0", offc1(y, h + X / 2, 8))
+        if h + X == 2:
+            for b in range(4):
+                mm(b, "e", 128 * (4 * y + b), "p2", 512 * y, 512, y == 0, y == 1)
+        if not pieces:
+            for b in range(4):
+                act(R("gs1", 512 * b, 512 * b + 512), R("ps%d" % b, 0, 512))
+
     tr(xu(), xk())
     for h in range(2):
         cp(ko(16 * h, 16 * h + 16), xu(32 * h, 32 * h + 16))
-    route(ko(), pre1, R("win0", WQ, WQ + 512), 1)
+    route(ko(), pre1, R("win0", WQ, WQ + 512), 1, piece)
     kw, jw, jl, o4 = new("rf", 2 * K), new("rf", K), new("rf", K), [new("ru", K) for t in range(4)]
     for j, to in ((1, kw(0, K)), (9, kw(K, 2 * K)), (0, jw())):
         dma("y", to, R("win1", 0, L, 1, (j, 128, 16)))
@@ -644,18 +666,24 @@ def rank_program(g, core, T, topo):
         cp(R("rq1", 0, 2 * K, 2), kw(0, K))
         cp(R("rq1", 1, 2 * K, 2), kw(K, 2 * K))
         ask(1, 12, "all1", 0, N - 1)
+
+    def own_list():
         ts(jl(), jw(), float(C * r), A.subtract, float(C - 1), A.min)
         for t in range(4):
             ts(o4[t](), jl(), 4.0, A.mult, float(t), A.add)
 
-    make(1, "a", offa1, lambda X: None, None, ask_k)
+    make(1, "a", offa1, lambda X: own_list() if X == 0 else None, None, ask_k)
     compose(1, lambda t: R("nt1"), lambda t, a, b: o4[t](a, b), "b1", lambda c, i0, i1: None,
-            {(0, 0): lambda: unwrap(1, ((1, 9),)), (1, 0): lambda: invert(1)})
+            {(0, 0): lambda: unwrap(1, ((1, 9),))})
+    invert(1)
     quant("b1", L, C, R("nt1"))
     y_part(7, 0, "a", C * r, 0, C)
     y_part(6, 1, "b1", L, 0, C)
     todo[1]()
-    offb2, offa2 = table(1, (0, 9), (L - C * r, 0), cp)()[1]
+    t1 = new("rf", 512)
+    tr(t1(), R("win1", WQ, WQ + 512))
+    offa2 = lists(lambda l, y: t1(16 * y + 9, 512, 32), [0], cp)[1][0]
+    offb2 = lists(lambda l, y: t1(16 * y, 512, 32), [L - C * r], act)[1][0]
     codes_out(1, "b1", L)
     dma("y", ext(T.y[:, 0:2 * C]), R("ysb", 0, 2 * C))
 

from concourse.bass import DstId, RemoteDMATransfer
from concourse.mybir import dt, AluOpType, ActivationFunctionType

N, C, S = 8, 256, 48
B = 2 * S
L = (N - 1) * B
K = L // 16
WQ = 2 * L
WIN = WQ + 512 + 32 + WQ + 32
PAD = 4096.0
F32, BF, I32, U16, X4, U8 = "float32", "bfloat16", "int32", "uint16", "float8_e4m3fn_x4", "uint8"
BYTES = {F32: 4, I32: 4, X4: 4, BF: 2, U16: 2, U8: 1}

SCRATCH = {}


def _sb(names, n, t):
    for x in names.split():
        SCRATCH[x] = ("sbuf", [128, n], t)


_sb("jn kn", 32, I32)
_sb("flat", 512, I32)
_sb("xbt xct xbp nt0 nt1 nt2 mt", 1024, BF)
_sb("vt zb", 512, BF)
_sb("gs0 gs1 gs2 pr", 2048, BF)
_sb("eb", 4 * 516, BF)
_sb("ct0 ct1", 4 * L, BF)
for _n, _w in (("w", 512), ("v", 128), ("e", 1024), ("c0", N * C), ("a", N * C), ("b0", L + C), ("b1", L + C), ("c1", C),
               ("m0", C), ("m1", C), ("m2", C), ("t0", L), ("t1", L),
               ("p0", 1024), ("p1", 1024), ("p2", 1024), ("p3", 1024), ("p4", 1024), ("p5", 1024)):
    _sb(_n + "q", _w, X4)
    _sb(_n + "z", _w, U8)
_sb("idt", 128, F32)
_sb("cf", 896, F32)
_sb("ci", 192, I32)
_sb("cu", 64, U16)
_sb("rf", 7168, F32)
_sb("ri", 1024, I32)
_sb("ru", 1024, U16)
_sb("win0 win1", WIN, F32)
_sb("wt0", WQ, F32)
_sb("fr0 fr1 fl0 fl1", L, F32)
_sb("rq0 rl0", 3 * K, F32)
_sb("rq1 rl1", 2 * K, U16)
_sb("ysb", 3 * C, F32)
for _k in range(8):
    SCRATCH["ps%d" % _k] = ("psum", [128, 512], F32)

ARR = ["c0q", "c0z", "aq", "az", "b0q", "b0z", "b1q", "b1z", "far0", "near0", "all1"]
SEMAPHORES = ["qv", "qs", "qt", "qg", "sent"] + ["in_" + x for x in ARR] + ["d%d" % k for k in range(40)]

A = AluOpType
COPY = ActivationFunctionType.Copy
IDENT = ActivationFunctionType.Identity
WAKE, LOCAL, REMOTE, FIRST, ROW, RATE, GATHER, SCATTER = 200.0, 1800.0, 2000.0, 2700.0, 15.0, 35.0, 1.45, 2.8


def rank_program(g, core, T, topo):
    r = T.rank_of(core)
    if r is None:
        return
    cores = T.cores

    def order(a):
        o = [x for x in range(N) if x != a]
        return [x for x in o if topo.die(cores[x]) != topo.die(cores[a])] + [x for x in o if topo.die(cores[x]) == topo.die(cores[a])]

    others = order(r)
    nx = len([x for x in others if topo.die(cores[x]) != topo.die(core)])
    eng = topo.engines(core, cores[others[0]])
    even, odd = eng[0::2], eng[1::2]

    Q = {"v": g.vector, "s": g.scalar, "t": g.tensor, "g": g, "y": g.sync}
    count, seen, log, ndma, nodes, tail, sent = {}, {}, {}, [0], [], {}, {}

    def R(name, a=None, b=None, s=1, p=None):
        if a is None:
            a, b = 0, T[name].shape[1]
        cs = slice(a, b, s) if s > 1 else slice(a, b)
        ap = T[name][:, cs] if p is None else T[name][slice(p[0], p[1], p[2]), cs]
        if name[:2] == "ps":
            return ap, [(name, 0, 512, 1, None, b - a)]
        return ap, [(name, a, b, s, p, (b - a + s - 1) // s)]

    def ext(ap):
        return ap, []

    def u8(x):
        return x[0].bitcast(dt.uint8), x[1]

    def u32(x):
        return x[0].bitcast(dt.uint32), x[1]

    def ind(w, o):
        return w[0].indirect(o[0]), w[1], o[1]

    def meet(x, y):
        if x[2] <= y[1] or y[2] <= x[1]:
            return False
        if x[3] > 1 and x[3] == y[3] and x[1] % x[3] != y[1] % y[3]:
            return False
        if x[4] and y[4] and not set(range(*x[4])) & set(range(*y[4])):
            return False
        return True

    def wait(q, tok):
        if seen.get((q, tok[0]), 0) < tok[1]:
            seen[(q, tok[0])] = tok[1]
            Q[q].wait_ge(T.sem[tok[0]], tok[1])

    def node(q, reads, writes, cost, lag, call, more=(), move=None):
        need, follow = set(more), set()
        for keys, w in ((reads, False), (writes, True)):
            for x in keys:
                for y, yw, i in log.get(x[0], []):
                    if meet(x, y) and (w or yw or (x[0][:2] == "ps" and nodes[i]["q"] != q)):
                        (follow if q == "t" and nodes[i]["q"] == "t" else need).add(i)
        if q in ("g", "y", "v"):
            if q in tail:
                follow.add(tail[q])
            tail[q] = len(nodes)
        nodes.append({"q": q, "cost": cost, "lag": lag, "need": need, "follow": follow, "call": call, "tok": None})
        if move:
            chain = {tail["e"]} if q == "g" and "e" in tail else set()
            if q == "g":
                tail["e"] = len(nodes)
            nodes.append({"q": "e", "cost": move, "lag": lag, "need": {len(nodes) - 1}, "follow": chain, "call": None, "tok": None})
        for keys, w in ((reads, False), (writes, True)):
            for x in keys:
                log.setdefault(x[0], []).append((x, w, len(nodes) - 1))
        return len(nodes) - 1

    def issue():
        far = [0.0] * len(nodes)
        for i in range(len(nodes) - 1, -1, -1):
            x = nodes[i]
            far[i] += x["cost"]
            for j in x["need"]:
                far[j] = max(far[j], far[i] + nodes[j]["lag"])
            for j in x["follow"]:
                far[j] = max(far[j], far[i])
        start = [-x for x in far]
        for turn in range(2):
            busy, rank = {}, list(start)
            for i in sorted(range(len(nodes)), key=lambda i: (rank[i], i)):
                x = nodes[i]
                t = max([0.0] + [start[j] + nodes[j]["cost"] + nodes[j]["lag"] for j in x["need"]]
                        + [start[j] + nodes[j]["cost"] for j in x["follow"] if turn == 0 or x["q"] != "v"])
                if x["q"] != "r":
                    slots = busy.setdefault(x["q"], [])
                    for a, b in slots:
                        if t + x["cost"] <= a:
                            break
                        t = max(t, b)
                    slots.append((t, t + x["cost"]))
                    slots.sort()
                start[i] = t
        for i in sorted(range(len(nodes)), key=lambda i: (start[i], i)):
            x = nodes[i]
            if x["q"] in ("r", "e"):
                continue
            need = {}
            for j in x["need"]:
                s, n = nodes[j]["tok"]
                need[s] = max(need.get(s, 0), n)
            for s in sorted(need):
                wait(x["q"], (s, need[s]))
            x["tok"] = x["call"]()
            if i + 1 < len(nodes) and nodes[i + 1]["q"] == "e":
                nodes[i + 1]["tok"] = x["tok"]
        for s in count:
            wait("g", (s, count[s]))

    def split(outs, ins):
        reads, writes = [], []
        for x in outs:
            writes += x[1]
            if len(x) > 2:
                reads += x[2]
        for x in ins:
            if isinstance(x, tuple):
                reads += x[1]
                if len(x) > 2:
                    reads += x[2]
        return reads, writes

    def ap(x):
        return x[0] if isinstance(x, tuple) else x

    def size(x):
        return x[1][0][5]

    def narrow(x):
        return SCRATCH[x[1][0][0]][2] == BF

    def run(q, outs, ins, call, per=1.0):
        reads, writes = split(outs, ins)
        if len(outs[0]) > 2:
            cost = 50 + SCATTER * size(ins[0])
        elif ins and len(ins[0]) > 2:
            cost = 55 + GATHER * size(outs[0])
        elif q == "v":
            cost = max(66.0, per * size(outs[0]) * (0.52 if per == 1.0 and narrow(outs[0]) and all(narrow(x) for x in ins[:1]) else 1.04))
        else:
            cost = {"s": 66, "g": 130, "t": 10}[q] + per * size(outs[0]) * 1.04

        def go():
            s = "q" + q
            count[s] = count.get(s, 0) + 1
            call().then_inc(T.sem[s], 1)
            return s, count[s]
        node(q, reads, writes, cost, WAKE, go)

    def dma(q, out, in_, behind=()):
        reads, writes = split([out], [in_] + list(behind))
        s = "d%d" % ndma[0]
        ndma[0] += 1

        def go():
            count[s] = 16
            Q[q].dma_start(out[0], in_[0]).then_inc(T.sem[s], 16)
            return s, 16
        x = out if out[1] else in_
        rows = 128 if not x[1][0][4] or x[1][0][4][2] > 1 else 16
        width = size(x) * BYTES[SCRATCH[x[1][0][0]][2]] * (len(range(*x[1][0][4])) if x[1][0][4] else 128)
        node(q, reads, writes, 60.0, LOCAL / 2, go, (), (rows * ROW + width / RATE) / 16)

    def cp(out, in_):
        run("v", [out], [in_], lambda: g.vector.tensor_copy(out[0], in_[0]))

    def tt(out, a, b, op):
        run("v", [out], [a, b], lambda: g.vector.tensor_tensor(out[0], a[0], b[0], op),
            1.0 if a[1][0][0][:2] == "ps" else (1.01 if narrow(out) else 2.0))

    def ts(out, a, s1, op0, s2=None, op1=None):
        if op1 is None:
            run("v", [out], [a, s1], lambda: g.vector.tensor_scalar(out[0], a[0], ap(s1), None, op0))
        else:
            run("v", [out], [a, s1, s2], lambda: g.vector.tensor_scalar(out[0], a[0], ap(s1), ap(s2), op0, op1))

    def scan(out, d0, d1, init, op0, op1):
        run("v", [out], [d0, d1, init], lambda: g.vector.tensor_tensor_scan(out[0], d0[0], d1[0], ap(init), op0, op1))

    def tr(out, in_):
        run("v", [out], [in_], lambda: g.vector.transpose(out[0], in_[0]))

    def fill(out, c):
        run("v", [out], [], lambda: g.vector.memset(out[0], c))

    def act(out, in_, scale=None):
        if scale is None:
            run("s", [out], [in_], lambda: g.scalar.activation(out[0], in_[0], COPY))
        else:
            f = IDENT if isinstance(scale, tuple) else COPY
            run("s", [out], [in_, scale], lambda: g.scalar.activation(out[0], in_[0], f, scale=ap(scale)))

    def sfill(name, n, c):
        for a in range(0, n, 512):
            o, z = R(name, a, min(n, a + 512)), R("zb", 0, min(n - a, 512))
            run("s", [o], [z], lambda o=o, z=z: g.scalar.activation(o[0], z[0], IDENT, bias=c))

    def iota(out, pattern, base, cm, real=False):
        if real:
            run("g", [out], [], lambda: g.iota(out[0], pattern, base, cm, allow_small_or_imprecise_dtypes=True), 2.0)
        else:
            run("g", [out], [], lambda: g.iota(out[0], pattern, base, cm), 2.0)

    def quant(name, a, n, tile):
        q, z = R(name + "q", a, a + n), R(name + "z", a, a + n)
        run("v", [q, z], [tile], lambda: g.vector.quantize_mx(q[0], z[0], tile[0]), 1.1)

    def mm(bank, wn, wa, xn, xa, n, start, stop):
        o = R("ps%d" % bank, 0, n)
        i = [R(wn + "q", wa, wa + 128), R(wn + "z", wa, wa + 128), R(xn + "q", xa, xa + n), R(xn + "z", xa, xa + n)]
        run("t", [o], i, lambda: g.tensor.matmul_mx(o[0], i[0][0], i[1][0], i[2][0], i[3][0], start, stop), 0.6)

    def bits(e):
        return sum(1 << x for x in e)

    def dst(x):
        rid, pid, se = topo.addr(cores[x])
        return DstId(rid=rid, pnc=pid)

    def send(sem, items):
        reads = []
        for x in items:
            reads += x[0][1]
        width = size(items[0][0]) * BYTES[SCRATCH[reads[0][0]][2]]
        cost = sum(len(x[1]) for x in items) * 128 * (ROW + width / RATE) / 14

        def go():
            moves = [RemoteDMATransfer(dst_ids=[dst(a) for a, d in to], dma_engine_mask=bits(e), remote_sem=T.sem["in_" + sem],
                                       srcs=[src[0]], dsts=[d[0] for a, d in to]) for src, to, e in items]
            g.remote_dma_fused(moves, local_sem=T.sem.sent)
            count["sent"] = count.get("sent", 0) + sum(len(x[2]) for x in items)
        cost0 = 300.0 + (0 if sent else FIRST)
        sent.setdefault(sem, []).append(node("g", reads, [], cost0, REMOTE / 2, go, (), cost))

    def lands(sem, name, ranges, n):
        count["in_" + sem] = n
        i = node("r", [], [(name, a, b, 1, None, b - a) for a, b in ranges], 1.0, 0.0, None, sent[sem])
        nodes[i]["tok"] = ("in_" + sem, n)

    def share(e, n):
        k = 1
        while 2 * k * n <= len(e):
            k *= 2
        return [e[k * i:k * i + k] for i in range(n)]

    def spread_codes(name):
        x = u8(R(name + "q", C * r, C * r + C))
        send(name + "q", [(x, [(a, x) for a in others[:nx]], even), (x, [(a, x) for a in others[nx:]], odd)])
        lands(name + "q", name + "q", [(C * a, C * a + C) for a in others], len(even) * (N - 1))

    def spread_scales(name):
        x = R(name + "z", C * r, C * r + C)
        send(name + "z", [(x, [(a, x) for a in others[:nx // 2]], even), (x, [(a, x) for a in others[nx // 2:]], odd)])
        lands(name + "z", name + "z", [(C * a, C * a + C) for a in others], len(even) * (N - 1))

    def place(a):
        return order(a).index(r)

    top = {"rf": 0, "ri": 0, "ru": 0, "cf": 0, "ci": 0, "cu": 0}

    def new(name, n):
        o = top[name]
        top[name] = o + (n + 31) // 32 * 32
        return lambda a=0, b=n, s=1: R(name, o + a, o + b, s)

    pcol = new("ci", 4)
    iota(pcol(0, 1), [[0, 1]], 0, 1)
    iota(R("idt"), [[-1, 128]], 0, 1, True)
    iota(R("flat"), [[1, 16], [0, 2], [16, 16]], C * r, 0)
    dma("y", R("jn"), ext(T.jb[:]))
    dma("s", R("xct"), ext(T.xc[:]))
    dma("y", R("flat", 0, 512, 1, (0, 128, 16)), ext(T.jb[:]))
    dma("y", R("flat", 0, 512, 1, (1, 128, 16)), ext(T.kc[:]))
    dma("y", R("xbt"), ext(T.xb[:]))
    dma("y", R("kn"), ext(T.kc[:]))
    dma("y", R("vt"), ext(T.v[:]))
    dma("y", u8(R("wq")), ext(T.wc[:]))
    dma("y", R("wz"), ext(T.ws[:]))
    W7 = 32 * (N - 1)
    r16, r7, zero, col = new("cf", W7), new("cf", W7), new("cf", 16), new("cf", 8)
    fill(R("zb"), 0.0)
    fill(r16(), 1.0)
    fill(r7(), 1.0)
    ts(pcol(1, 2), pcol(0, 1), 31, A.bitwise_and)
    ts(pcol(2, 3), pcol(0, 1), 16, A.bitwise_and)
    ts(pcol(3, 4), pcol(0, 1), 15, A.bitwise_and)
    fill(zero(), 0.0)
    fill(r16(0, W7, 16), 0.0)
    fill(r7(0, W7, N - 1), 0.0)
    m0, m1, g16, base, own0, own1, p32, pk = [col(k, k + 1) for k in range(8)]
    ts(m0, pcol(2, 3), 0.0, A.is_equal)
    ts(m1, pcol(2, 3), 16.0, A.is_equal)
    cp(g16, pcol(2, 3))
    cp(p32, pcol(1, 2))
    ts(base, pcol(1, 2), float(S), A.mult, -1.0, A.add)
    ts(own0, pcol(2, 3), -1.0, A.mult, float(WQ), A.add)
    ts(own1, pcol(2, 3), -1.0, A.mult, float(WQ + 16), A.add)
    ts(pk, pcol(3, 4), float(K), A.mult)
    ident = new("cf", 128)
    sfill("win0", WQ, PAD)
    sfill("eb", 4 * 516, 0.0)
    sfill("fr0", L, 0.0)
    sfill("win1", L, PAD)

    def ready():
        tot, u = new("rf", 32), new("rf", 32)
        fill(tot(), 0.0)
        cp(u(0, 1), base)
        cp(u(16, 17), base)
        return tot, u

    def route(jo, pre, vals, k, more=lambda: None):
        tot, u = pre
        o, x, hi, pi, t, t2 = [new("ri", 32) for i in range(6)]
        h, s1, h2, s2, w, w2 = [new("rf", W7) for i in range(6)]
        ho, a1, a2, a3, a4, a5, tt_, ut, uu, ad = [new("rf", 32) for i in range(10)]
        off = new("ru", 32)
        ts(o(), jo, 8, A.arith_shift_right)
        ts(x(), jo, C - 1, A.bitwise_and)
        for i, a in enumerate(others):
            ts(h(32 * i, 32 * i + 32), o(), float(a), A.is_equal)
        ts(hi(), x(), 4, A.arith_shift_right)
        scan(s1(), r16(), h(), 0.0, A.mult, A.add)
        ts(ho(), o(), float(r), A.is_equal)
        cp(tot(0, 2 * N - 2), s1(15, W7, 16))
        ts(a1(0, 16), x(0, 16), 32.0, A.mult, own0 if k == 0 else float(WQ), A.add)
        more()
        tr(tt_(), tot())
        more()
        ts(a1(16, 32), x(16, 32), 32.0, A.mult, own1 if k == 0 else float(WQ + 16), A.add)
        scan(u(1, 16), tt_(0, 15), zero(0, 15), base, A.add, A.add)
        scan(u(17, 32), tt_(16, 31), zero(0, 15), base, A.add, A.add)
        cp(h2(), h())
        tr(ut(), u())
        more()
        ts(a2(), hi(), -511.0, A.mult)
        tt(h2(0, W7, 16), h(0, W7, 16), ut(0, 2 * N - 2), A.add)
        tt(a3(), a1(), a2(), A.add)
        more()
        scan(s2(), r16(), h2(), 0.0, A.mult, A.add)
        tt(a4(), a3(), ho(), A.mult)
        more()
        for i in range(N - 1):
            tt(w(i, W7, N - 1), s2(32 * i, 32 * i + 32), h(32 * i, 32 * i + 32), A.mult)
        scan(w2(), r7(), w(), 0.0, A.mult, A.add)
        p = w2(N - 2, W7, N - 1)
        more()
        cp(pi(), p)
        more()
        if k == 1:
            ts(t(), pi(), 15, A.bitwise_and)
            ts(t2(), pi(), 4, A.arith_shift_right)
            ts(a5(), t(), float(K), A.mult)
            tt(uu(), t2(), a4(), A.add)
            tt(ad(), a5(), uu(), A.add)
            more()
            cp(off(0, 32, 2), ad(0, 16))
            cp(off(1, 32, 2), ad(16, 32))
        else:
            tt(uu(), p, a4(), A.add)
            ts(t(), pi(), 0x7FF0, A.bitwise_and)
            tt(ad(), t(), uu(), A.add)
            ts(off(0, 32, 2), ad(0, 16), g16, A.add)
            ts(off(1, 32, 2), ad(16, 32), g16, A.add)
        cp(ind(R("win%d" % k, 0, WQ + 512), off()), vals)
        return p, x, ho

    def ask(k, n, sem, i0, i1):
        e = share(eng, i1 - i0)
        send(sem, [(R("rq%d" % k, n * i, n * i + n), [(others[i], R("rl%d" % k, n * place(others[i]), n * place(others[i]) + n))], e[i - i0])
                   for i in range(i0, i1)])
        lands(sem, "rl%d" % k, [(n * i0, n * i1)], len(e[0]) * (i1 - i0))

    def unwrap(k, rows):
        for l, j in rows:
            x = new("rf", K)
            cp(x(), R("rl%d" % k, l, (3 - k) * K, 3 - k))
            dma("y", R("fr%d" % k, 0, L, 1, (j, 128, 16)), x())

    todo = {}

    def invert(k):
        act(R("fl%d" % k), ind(R("fr%d" % k), turn()))
        x, hi = new("ri", K), new("ri", K)
        a1, a2, mk, md, a3, a4, a5 = [new("rf", K) for i in range(7)]
        off = new("ru", K)
        rl = R("rl%d" % k, 0, (3 - k) * K, 3 - k)
        ts(x(), rl, float(C * r), A.subtract, float(C - 1), A.min)
        ts(mk(), rl, float(N * C), A.is_ge)
        ts(hi(), x(), 4, A.arith_shift_right)
        ts(a1(), x(), 32.0, A.mult)
        tt(md(), mk(), behind(), A.mult)
        ts(a2(), hi(), -511.0, A.mult)
        tt(a4(), md(), half16(), A.add)
        tt(a3(), a1(), a2(), A.add)
        tt(a5(), a3(), a4(), A.add)
        cp(off(), a5())
        todo[k] = lambda: cp(ind(R("win%d" % k, WQ, WIN), off()), R("fl%d" % k))

    def lists(src, adds, move):
        n = 64 * len(adds)
        z, d, u = new("rf", n), new("rf", n), new("ru", n)
        for l in range(len(adds)):
            for y in range(2):
                for e in range(2):
                    a = 64 * l + 32 * y + 16 * e
                    move(z(a, a + 16), src(l, y))
        tr(d(), z())
        for l, c in enumerate(adds):
            ts(u(64 * l, 64 * l + 64), d(64 * l, 64 * l + 64), float(c), A.add)
        return d, [(lambda y, h, n=16, l=l: u(64 * l + 32 * y + int(16 * h), 64 * l + 32 * y + int(16 * h) + n)) for l in range(len(adds))]

    def table(k, rows, adds, move):
        t1 = new("rf", 512)
        tr(t1(), R("win%d" % k, WQ, WQ + 512))
        return lambda: lists(lambda l, y: t1(16 * y + rows[l], 512, 32), adds, move)

    def pick(dn, a, n, sn, off):
        w = T[sn + "q"].shape[1]
        cp(u32(R(dn + "q", a, a + n)), ind(u32(R(sn + "q", 0, w)), off))
        act(R(dn + "z", a, a + n), ind(R(sn + "z", 0, w), off))

    def early(mode, sn, off):
        dn = "p%d" % (2 * mode)
        for y in range(2):
            pick(dn, 512 * y, 512, sn, off(y, 0, 32))
            for b in range(4):
                mm(b, "e", 128 * (4 * y + b), dn, 512 * y, 512, y == 0, y == 1)
        for b in range(4):
            act(R("gs%d" % mode, 512 * b, 512 * b + 512), R("ps%d" % b, 0, 512))

    def make(mode, sn, off, done, other=None, middle=None):
        dn, gs, mn, nt = "p%d" % (2 * mode + 1), "gs%d" % mode, "m%d" % mode, "nt%d" % mode

        def unpack(dn, sn, off, h, bank):
            for y in range(2):
                pick(dn, 512 * y + 256 * h, 256, sn, off(y, h))
                for b in range(4):
                    mm(bank + b, "e", 128 * (4 * y + b), dn, 512 * y + 256 * h, 256, y == 0, y == 1)

        def times(h, bank):
            for b in range(4):
                tt(R("pr", 1024 * h + b, 1024 * h + 1024, 4), R("ps%d" % (bank + b), 0, 256),
                   R(gs, 512 * b + 256 * h, 512 * b + 256 * h + 256), A.mult)

        if other:
            for h in range(2):
                unpack("p%d" % (2 * mode), other[0], other[1], h, 0)
                for b in range(2 * h, 4):
                    act(R(gs, 512 * b + 256 * h, 512 * b + 256 * h + 256), R("ps%d" % b, 0, 256))
        unpack(dn, sn, off, 0, 4)
        for b in range(2 if other else 0):
            cp(R(gs, 512 * b + 256, 512 * b + 512), R("ps%d" % b, 0, 256))
        unpack(dn, sn, off, 1, 0)
        times(0, 4)
        if middle:
            middle()
        times(1, 0)
        for X in range(2):
            a = 512 * X
            tt(R("mt", a, a + 512), R("pr", a, a + 512), R("pr", 1024 + a, 1536 + a), A.add)
            quant(mn, 128 * X, 128, R("mt", a, a + 512))
            for b in range(4):
                mm(4 - 4 * X + b, "w", 128 * b, mn, 128 * X, 128, True, True)
            if X == 0:
                for b in range(4):
                    act(R(nt, b, 512, 4), R("ps%d" % (4 + b), 0, 128), 0.03125)
        done(0)
        for b in range(2):
            ts(R(nt, 512 + b, 1024, 4), R("ps%d" % b, 0, 128), 0.03125, A.mult)
            act(R(nt, 514 + b, 1024, 4), R("ps%d" % (2 + b), 0, 128), 0.03125)
        done(1)

    def compose(k, win, off, land, ahead, meanwhile):
        ct, tn = "ct%d" % k, "t%d" % k
        ec = [share(even, nx), share(eng, N - 1 - nx)]
        ez = [share(odd, nx), share(eng[::-1], N - 1 - nx)]
        for c, (i0, i1) in enumerate(((0, nx), (nx, N - 1))):
            ahead(c, i0, i1)
            for t in range(4):
                (cp if t < 2 else act)(R(ct, 4 * B * i0 + t, 4 * B * i1, 4), ind(win(t), off(t, 6 * i0, 6 * i1)))
                meanwhile.get((c, t), lambda: None)()
            quant(tn, B * i0, B * (i1 - i0), R(ct, 4 * B * i0, 4 * B * i1))
            for z, e, f in (("q", ec[c], u8), ("z", ez[c], lambda x: x)):
                send(land + z, [(f(R(tn + z, B * i, B * i + B)),
                                 [(others[i], f(R(land + z, B * place(others[i]), B * place(others[i]) + B)))], e[i - i0])
                                for i in range(i0, i1)])
        for z, e in (("q", ec), ("z", ez)):
            lands(land + z, land + z, [(0, L)], nx * len(e[0][0]) + (N - 1 - nx) * len(e[1][0]))

    def codes_out(f, name, at):
        dma("y", ext(T.oc[:, 4 * C * f:4 * C * f + 4 * C]), u8(R(name + "q", at, at + C)), [R(name + "q"), R(name + "z")])
        for k in range(4):
            dma("y", ext(T.osc[4 * k:4 * k + 4, C * f:C * f + C]), R(name + "z", at, at + C, 1, (32 * k, 32 * k + 4, 1)))

    def y_part(bank, f, name, at, a, n):
        mm(bank, "v", 0, name, at + a, n, True, True)
        act(R("ysb", C * f + a, C * f + a + n), R("ps%d" % bank, 0, n))

    def y_out(f, q):
        dma(q, ext(T.y[:, C * f:C * f + C]), R("ysb", C * f, C * f + C))

    pre0 = ready()
    ts(ident(), R("idt"), 0.0, A.is_equal)
    xj, xt, jo = new("rf", 64), new("rf", 64), new("ri", 32)
    for h in range(2):
        ts(xj(32 * h, 32 * h + 16), R("jn", 16 * h, 16 * h + 16), m0, A.mult)
        ts(xj(32 * h + 16, 32 * h + 32), R("jn", 16 * h, 16 * h + 16), m1, A.mult)
    tr(xt(), xj())
    for h in range(2):
        tt(jo(16 * h, 16 * h + 16), xt(32 * h, 32 * h + 16), xt(32 * h + 16, 32 * h + 32), A.add)
    quant("c0", C * r, C, R("xct"))
    spread_codes("c0")
    spread_scales("c0")
    c32, c1, half16, behind, turn = new("ci", K), new("ci", K), new("cf", K), new("cf", K), new("cu", K)
    iota(c32(), [[32, K]], 0, 0)
    iota(c1(), [[1, K]], 0, 0)
    iota(half16(), [[0, N - 1], [16, 2], [0, 3]], 0, 0, True)
    p, x, ho = route(jo(), pre0, R("flat"), 0)
    for sem, i0, i1 in (("far0", 0, nx), ("near0", nx, N - 1)):
        a, b = 2 * B * i0, 2 * B * i1
        tr(R("wt0", a, b), R("win0", a, b))
        for l, j in enumerate((0, 1, 9)):
            tt(R("rq0", 18 * i0 + l, 18 * i1, 3), R("wt0", a + j, b, 32), R("wt0", a + 16 + j, b, 32), A.min)
        ask(0, 18, sem, i0, i1)
    iota(R("fr1"), [[1, 16], [16, K]], C * r - L, 0, True)
    for t in range(4):
        act(R("xbp", C * t, C * t + C), R("xbt", t, 4 * C, 4))
    ts(turn(), c1(), pk, A.add)
    ts(behind(), c32(), p32, A.add, 32.0, A.add)

    po, pa, z, d, u = new("rf", 32), new("rf", 32), new("rf", 64), new("rf", 64), new("ru", 64)
    kf, kt = new("rf", 32), new("rf", 32)
    ts(po(), x(), float(L), A.add)
    cp(kf(), R("kn"))
    tt(po(), po(), ho(), A.mult)
    tr(kt(), kf())
    tt(pa(), po(), p, A.add)
    offc0 = lists(lambda l, y: kt(16 * y, 16 * y + 16), [0], act)[1][0]
    for h in range(2):
        for e in range(2):
            act(z(32 * h + 16 * e, 32 * h + 16 * e + 16), pa(16 * h, 16 * h + 16))
    tr(d(), z())
    for y, m in enumerate((m0, m1)):
        for e in range(2):
            a = 516 * (2 * y + e)
            act(R("eb", a + 2 + e, a + 514, 4), ident(), m)
    cp(u(), d())
    offb0 = lambda y, h: u(32 * h + 16 * y, 32 * h + 16 * y + 16)
    for y in range(2):
        for b in range(4):
            a = 516 * (2 * y + b % 2) + (2 if b < 2 else 0)
            quant("e", 128 * (4 * y + b), 128, R("eb", a, a + 512))

    og = new("ru", K)

    def wanted(c, i0, i1):
        ts(og(6 * i0, 6 * i1), R("rl0", 18 * i0, 18 * i1, 3), float(C * r), A.subtract, float(C - 1), A.min)

    compose(0, lambda t: R("xbp", C * t, C * t + C), lambda t, a, b: og(a, b), "b0", wanted,
            {(0, 1): lambda: unwrap(0, ((0, 0), (1, 1), (2, 9)))})
    invert(0)
    quant("b0", L, C, R("xbt"))
    quant("v", 0, 128, R("vt"))
    early(0, "c0", offc0)
    todo[0]()
    rest = table(0, (9, 1), (0, 0), act)

    make(0, "b0", offb0, lambda X: quant("a", C * r + 128 * X, 128, R("nt0", 512 * X, 512 * X + 512)))
    spread_codes("a")
    spread_scales("a")
    d2, (offa1, offc1) = rest()

    pre1 = ready()
    xk, xu, ko = new("rf", 64), new("rf", 64), new("ri", 32)
    for h in range(2):
        for y in range(2):
            act(xk(32 * h + 16 * y, 32 * h + 16 * y + 16), d2(64 + 32 * y + 16 * h, 64 + 32 * y + 16 * h + 16))
    pieces = [(y, h, X) for y in range(2) for h in range(2) for X in range(2)]

    def piece():
        y, h, X = pieces.pop(0)
        pick("p2", 512 * y + 256 * h + 128 * X, 128, "c0", offc1(y, h + X / 2, 8))
        if h + X == 2:
            for b in range(4):
                mm(b, "e", 128 * (4 * y + b), "p2", 512 * y, 512, y == 0, y == 1)
        if not pieces:
            for b in range(4):
                act(R("gs1", 512 * b, 512 * b + 512), R("ps%d" % b, 0, 512))

    tr(xu(), xk())
    for h in range(2):
        cp(ko(16 * h, 16 * h + 16), xu(32 * h, 32 * h + 16))
    route(ko(), pre1, R("win0", WQ, WQ + 512), 1, piece)
    kw, jw, jl, o4 = new("rf", 2 * K), new("rf", K), new("rf", K), [new("ru", K) for t in range(4)]
    for j, to in ((1, kw(0, K)), (9, kw(K, 2 * K)), (0, jw())):
        dma("y", to, R("win1", 0, L, 1, (j, 128, 16)))
    codes_out(0, "a", C * r)

    def ask_k():
        cp(R("rq1", 0, 2 * K, 2), kw(0, K))
        cp(R("rq1", 1, 2 * K, 2), kw(K, 2 * K))
        ask(1, 12, "all1", 0, N - 1)

    def own_list():
        ts(jl(), jw(), float(C * r), A.subtract, float(C - 1), A.min)
        for t in range(4):
            ts(o4[t](), jl(), 4.0, A.mult, float(t), A.add)

    make(1, "a", offa1, lambda X: own_list() if X == 0 else None, None, ask_k)
    compose(1, lambda t: R("nt1"), lambda t, a, b: o4[t](a, b), "b1", lambda c, i0, i1: None,
            {(0, 0): lambda: unwrap(1, ((1, 9),))})
    invert(1)
    quant("b1", L, C, R("nt1"))
    y_part(7, 0, "a", C * r, 0, C)
    y_part(6, 1, "b1", L, 0, C)
    todo[1]()
    t1 = new("rf", 512)
    tr(t1(), R("win1", WQ, WQ + 512))
    offa2 = lists(lambda l, y: t1(16 * y + 9, 512, 32), [0], cp)[1][0]
    offb2 = lists(lambda l, y: t1(16 * y, 512, 32), [L - C * r], act)[1][0]
    codes_out(1, "b1", L)
    dma("y", ext(T.y[:, 0:2 * C]), R("ysb", 0, 2 * C))

    def last(X):
        quant("c1", 128 * X, 128, R("nt2", 512 * X, 512 * X + 512))
        y_part(5 + X, 2, "c1", 0, 128 * X, 128)

    make(2, "b1", offb2, last, ("a", offa2))
    codes_out(2, "c1", 0)
    y_out(2, "s")

    issue()
